import numpy as np
import ml_dtypes


def mxq(x, axis, fmt="e4m3"):
    dtype, down = {"e4m3": (ml_dtypes.float8_e4m3fn, 7), "e5m2": (ml_dtypes.float8_e5m2, 14)}[fmt]
    v = np.moveaxis(np.asarray(x, np.float32).astype(ml_dtypes.bfloat16).astype(np.float64), axis, -1)
    blocks = v.reshape(v.shape[:-1] + (-1, 32))
    amax = np.abs(blocks).max(-1, keepdims=True)
    byte = np.maximum(np.where(amax > 0, np.frexp(amax)[1] - 1 + 127, 0) - down, 1)
    scale = np.exp2(byte - 127.0)
    codes = (blocks / scale).astype(np.float32).astype(dtype).astype(np.float64)
    return np.moveaxis((codes * scale).reshape(v.shape), -1, axis)


WIDE = False


def mx_kscale(k):
    if not WIDE:
        return np.ones(k)
    levels = np.array([10, -10, 5, -5, 0])
    if k % 512:
        return np.exp2(np.random.permutation(np.resize(levels, k // 32))).repeat(32)
    a = np.empty((k // 512, 16))
    for p in range(k // 512):
        a[p, :8] = np.random.permutation(np.resize(levels, 8))
        for g in range(8):
            far = levels[np.abs(levels - a[p, g]) >= 10]
            a[p, g + 8] = far[np.random.randint(len(far))]
    return np.exp2(a.ravel()).repeat(32)


def f64(x):
    return np.asarray(x).astype(np.float64)


def striped(idx):
    return np.tile(idx.reshape(-1, 16).T, (8, 1)).astype(np.uint16)


def unstriped(offs):
    return offs[:16].T.reshape(-1).astype(np.int64)


K, T, E, C, N = 1536, 2048, 16, 128, 128


def by_expert(wq, xq):
    return np.concatenate([wq[e].T @ xq[:, e * C:(e + 1) * C] for e in range(E)], axis=1)


def setup_inputs():
    n = np.random.standard_normal
    s = mx_kscale(K)[:, None]
    return {
        "xT": (n((K, T)) * s).astype(np.float32),
        "w": (n((E, K, N)) / np.sqrt(K) / s[None]).astype(np.float32),
        "b": (0.3 * n((N, E))).astype(np.float32),
        "gate": np.tile(np.random.uniform(0.2, 1.0, E * C), (N, 1)).astype(np.float32),
        "offs": striped(np.random.permutation(T)[:E * C]),
    }


def reference(xT, w, b, gate, offs):
    idx = unstriped(offs)
    xq = mxq(f64(xT)[:, idx], 0, "e4m3")
    y = by_expert(mxq(f64(w), 1, "e4m3"), xq)
    y = y + np.repeat(f64(b), C, axis=1)
    out = np.zeros((N, T))
    out[:, idx] = f64(gate) * y
    return out

@@ -1,0 +1,129 @@
+from contextlib import ExitStack
+
+import concourse.mybir as mybir
+
+K, T, E, C, N = 1536, 2048, 16, 128, 128
+FLOPS = 2 * K * T * N
+
+F32 = mybir.dt.float32
+BF16 = mybir.dt.bfloat16
+U32 = mybir.dt.uint32
+U16 = mybir.dt.uint16
+U8 = mybir.dt.uint8
+FP8X4 = mybir.dt.float8_e4m3fn_x4
+ADD, MULT = mybir.AluOpType.add, mybir.AluOpType.mult
+
+P = 128
+PACK = 4
+K_PASS = P * PACK
+PASSES = K // K_PASS
+UNIT = 512
+CHUNKS = ((512, 512, 1024), (1024, 1024), (1024, 512, 512))
+X_VECTOR = {(0, 1), (1, 1), (2, 3)}
+W_VECTOR = {15}
+GATHER = 1024
+
+
+def tile_routed_moe_kernel(tc, xT, w, b, gate, offs, out):
+    nc = tc.nc
+    with ExitStack() as ctx:
+        keep = ctx.enter_context(tc.tile_pool(name="keep", bufs=1))
+        raws = ctx.enter_context(tc.tile_pool(name="raws", bufs=5))
+        halves = ctx.enter_context(tc.tile_pool(name="halves", bufs=4))
+        sums = ctx.enter_context(tc.psum_pool(name="sums", bufs=4))
+        ys = ctx.enter_context(tc.tile_pool(name="ys", bufs=3))
+
+        slots = keep.tile([P, T // 16], U16)
+        nc.sync.dma_start(slots[:], offs)
+        x_codes = [keep.tile([P, T], U32, name=f"x_codes{a}", align_bytes=64) for a in range(PASSES)]
+        x_scales = keep.tile([P, T], U8, align_bytes=64)
+        g_codes = [keep.tile([P, T], U32, name=f"g_codes{a}", align_bytes=64) for a in range(PASSES)]
+        g_scales = keep.tile([P, T], U8, align_bytes=64)
+        nc.gpsimd.memset(x_scales[:], 0)
+        bias = keep.tile([P, E], F32)
+        gates = keep.tile([P, E * C], F32)
+        result = keep.tile([P, T], F32)
+
+        def gather(out_tile, window):
+            for s in range(0, T, GATHER):
+                nc.vector.tensor_copy(
+                    out=out_tile[:, s : s + GATHER],
+                    in_=window[:].indirect(slots[:, s // 16 : (s + GATHER) // 16]),
+                )
+
+        for a in range(PASSES):
+            rows = xT[a * K_PASS : (a + 1) * K_PASS, :].rearrange("(p j) n -> p j n", j=PACK)
+            t0 = 0
+            for width in CHUNKS[a]:
+                raw = raws.tile([P, PACK, width], F32, name="raw")
+                nc.sync.dma_start(raw[:], rows[:, :, t0 : t0 + width])
+                for o in range(0, width, UNIT):
+                    half = halves.tile([P, UNIT, PACK], BF16, name="half", align_bytes=64)
+                    src = raw[:, :, o : o + UNIT].rearrange("p j n -> p n j")
+                    if (a, (t0 + o) // UNIT) in X_VECTOR:
+                        nc.vector.tensor_copy(out=half[:], in_=src)
+                    else:
+                        nc.scalar.copy(out=half[:], in_=src)
+                    cols = slice(t0 + o, t0 + o + UNIT)
+                    nc.vector.quantize_mx(
+                        out=x_codes[a][:, cols].bitcast(FP8X4),
+                        scales=x_scales[4 * a :, cols],
+                        in_=half[:].rearrange("p n j -> p (n j)"),
+                    )
+                t0 += width
+            gather(g_codes[a], x_codes[a])
+        gather(g_scales, x_scales)
+        nc.sync.dma_start(bias[:], b)
+        nc.sync.dma_start(gates[:], gate)
+
+        for e0 in range(0, E, 2):
+            raw = raws.tile([P, 2, PASSES, PACK, N], F32, name="raw")
+            half = halves.tile([P, 2, PASSES, N, PACK], BF16, name="half", align_bytes=64)
+            w_codes = keep.tile([P, 2, PASSES, N], U32, name=f"w_codes{e0}", align_bytes=64)
+            w_scales = keep.tile([P, 2, PASSES, N], U8, name=f"w_scales{e0}", align_bytes=64)
+            for i in range(2):
+                nc.sync.dma_start(
+                    raw[:, i, :, :, :].rearrange("p a j n -> p a (j n)"),
+                    w[e0 + i, :, :].rearrange("(a p j) n -> p a (j n)", p=P, j=PACK),
+                )
+                src = raw[:, i, :, :, :].rearrange("p a j n -> p a n j")
+                if e0 + i in W_VECTOR:
+                    nc.vector.tensor_copy(out=half[:, i, :, :, :], in_=src)
+                else:
+                    nc.scalar.copy(out=half[:, i, :, :, :], in_=src)
+            flat = half[:].rearrange("p i a n j -> p (i a n j)")
+            codes = w_codes[:].rearrange("p i a n -> p (i a n)")
+            scales = w_scales[:].rearrange("p i a n -> p (i a n)")
+            for c0, c1 in ((0, 512), (512, 768)):
+                nc.vector.quantize_mx(
+                    out=codes[:, c0:c1].bitcast(FP8X4),
+                    scales=scales[:, c0:c1],
+                    in_=flat[:, PACK * c0 : PACK * c1],
+                )
+            acc = sums.tile([P, 2, C], F32)
+            y = ys.tile([P, 2 * C], F32)
+            for i in range(2):
+                cols = slice((e0 + i) * C, (e0 + i + 1) * C)
+                for a in range(PASSES):
+                    nc.tensor.matmul_mx(
+                        out=acc[:, i, :],
+                        lhsT=w_codes[:, i, a, :].bitcast(FP8X4),
+                        lhsT_scale=w_scales[:, i, a, :],
+                        rhs=g_codes[a][:, cols].bitcast(FP8X4),
+                        rhs_scale=g_scales[4 * a :, cols],
+                        start=(a == 0),
+                        stop=(a == PASSES - 1),
+                    )
+                nc.vector.scalar_tensor_tensor(
+                    out=y[:, i * C : (i + 1) * C],
+                    in0=acc[:, i, :],
+                    scalar=bias[:, e0 + i : e0 + i + 1],
+                    in1=gates[:, cols],
+                    op0=ADD,
+                    op1=MULT,
+                )
+            nc.vector.tensor_copy(
+                out=result[:].indirect(slots[:, e0 * C // 16 : (e0 + 2) * C // 16]),
+                in_=y[:],
+            )
+        nc.sync.dma_start(out, result[:])

@@ -11,17 +11,22 @@ U32 = mybir.dt.uint32
 U16 = mybir.dt.uint16
 U8 = mybir.dt.uint8
 FP8X4 = mybir.dt.float8_e4m3fn_x4
-ADD, MULT = mybir.AluOpType.add, mybir.AluOpType.mult
+MULT = mybir.AluOpType.mult
 
 P = 128
 PACK = 4
+LINE = 4
 K_PASS = P * PACK
 PASSES = K // K_PASS
 UNIT = 512
-CHUNKS = ((512, 512, 1024), (1024, 1024), (1024, 512, 512))
-X_VECTOR = {(0, 1), (1, 1), (2, 3)}
-W_VECTOR = {15}
+CHUNKS = ((512, 512, 512, 512), (1024, 1024), (1024, 512, 512))
+X_VECTOR = {(0, 1), (0, 3), (1, 3), (2, 3)}
+W_VECTOR = set()
 GATHER = 1024
+GATE_COLS = 1024
+GATES_AFTER = {6: (0,), 10: (1,)}
+BIAS_AFTER = {10: (0, 12), 14: (12, 16)}
+LAG = {10: 0, 14: 0}
 
 
 def tile_routed_moe_kernel(tc, xT, w, b, gate, offs, out):
@@ -29,9 +34,9 @@ def tile_routed_moe_kernel(tc, xT, w, b, gate, offs, out):
     with ExitStack() as ctx:
         keep = ctx.enter_context(tc.tile_pool(name="keep", bufs=1))
         raws = ctx.enter_context(tc.tile_pool(name="raws", bufs=5))
-        halves = ctx.enter_context(tc.tile_pool(name="halves", bufs=4))
-        sums = ctx.enter_context(tc.psum_pool(name="sums", bufs=4))
-        ys = ctx.enter_context(tc.tile_pool(name="ys", bufs=3))
+        halves = ctx.enter_context(tc.tile_pool(name="halves", bufs=6))
+        sums = ctx.enter_context(tc.psum_pool(name="sums", bufs=8))
+        ys = ctx.enter_context(tc.tile_pool(name="ys", bufs=8))
 
         slots = keep.tile([P, T // 16], U16)
         nc.sync.dma_start(slots[:], offs)
@@ -40,16 +45,15 @@ def tile_routed_moe_kernel(tc, xT, w, b, gate, offs, out):
         g_codes = [keep.tile([P, T], U32, name=f"g_codes{a}", align_bytes=64) for a in range(PASSES)]
         g_scales = keep.tile([P, T], U8, align_bytes=64)
         nc.gpsimd.memset(x_scales[:], 0)
-        bias = keep.tile([P, E], F32)
+        biases = {e0: keep.tile([P, i1 - i0], F32, name=f"bias{e0}") for e0, (i0, i1) in BIAS_AFTER.items()}
         gates = keep.tile([P, E * C], F32)
         result = keep.tile([P, T], F32)
 
-        def gather(out_tile, window):
-            for s in range(0, T, GATHER):
-                nc.vector.tensor_copy(
-                    out=out_tile[:, s : s + GATHER],
-                    in_=window[:].indirect(slots[:, s // 16 : (s + GATHER) // 16]),
-                )
+        def gather(out_tile, window, s):
+            nc.vector.tensor_copy(
+                out=out_tile[:, s : s + GATHER],
+                in_=window[:].indirect(slots[:, s // 16 : (s + GATHER) // 16]),
+            )
 
         for a in range(PASSES):
             rows = xT[a * K_PASS : (a + 1) * K_PASS, :].rearrange("(p j) n -> p j n", j=PACK)
@@ -59,11 +63,12 @@ def tile_routed_moe_kernel(tc, xT, w, b, gate, offs, out):
                 nc.sync.dma_start(raw[:], rows[:, :, t0 : t0 + width])
                 for o in range(0, width, UNIT):
                     half = halves.tile([P, UNIT, PACK], BF16, name="half", align_bytes=64)
-                    src = raw[:, :, o : o + UNIT].rearrange("p j n -> p n j")
+                    src = raw[:, :, o : o + UNIT].rearrange("p j (c i) -> p c j i", i=LINE)
+                    dst = half[:].rearrange("p (c i) j -> p c j i", i=LINE)
                     if (a, (t0 + o) // UNIT) in X_VECTOR:
-                        nc.vector.tensor_copy(out=half[:], in_=src)
+                        nc.vector.tensor_copy(out=dst, in_=src)
                     else:
-                        nc.scalar.copy(out=half[:], in_=src)
+                        nc.scalar.copy(out=dst, in_=src)
                     cols = slice(t0 + o, t0 + o + UNIT)
                     nc.vector.quantize_mx(
                         out=x_codes[a][:, cols].bitcast(FP8X4),
@@ -71,12 +76,19 @@ def tile_routed_moe_kernel(tc, xT, w, b, gate, offs, out):
                         in_=half[:].rearrange("p n j -> p (n j)"),
                     )
                 t0 += width
-            gather(g_codes[a], x_codes[a])
-        gather(g_scales, x_scales)
-        nc.sync.dma_start(bias[:], b)
-        nc.sync.dma_start(gates[:], gate)
+            if a < PASSES - 1:
+                for s in range(0, T, GATHER):
+                    gather(g_codes[a], x_codes[a], s)
+        for s in range(0, T, GATHER):
+            gather(g_codes[PASSES - 1], x_codes[PASSES - 1], s)
+            gather(g_scales, x_scales, s)
 
-        for e0 in range(0, E, 2):
+        def bias_of(e):
+            for key, (i0, i1) in BIAS_AFTER.items():
+                if i0 <= e < i1:
+                    return biases[key][:, e - i0 : e - i0 + 1]
+
+        def prepare(e0):
             raw = raws.tile([P, 2, PASSES, PACK, N], F32, name="raw")
             half = halves.tile([P, 2, PASSES, N, PACK], BF16, name="half", align_bytes=64)
             w_codes = keep.tile([P, 2, PASSES, N], U32, name=f"w_codes{e0}", align_bytes=64)
@@ -86,11 +98,12 @@ def tile_routed_moe_kernel(tc, xT, w, b, gate, offs, out):
                     raw[:, i, :, :, :].rearrange("p a j n -> p a (j n)"),
                     w[e0 + i, :, :].rearrange("(a p j) n -> p a (j n)", p=P, j=PACK),
                 )
-                src = raw[:, i, :, :, :].rearrange("p a j n -> p a n j")
+                src = raw[:, i, :, :, :].rearrange("p a j (c i) -> p a c j i", i=LINE)
+                dst = half[:, i, :, :, :].rearrange("p a (c i) j -> p a c j i", i=LINE)
                 if e0 + i in W_VECTOR:
-                    nc.vector.tensor_copy(out=half[:, i, :, :, :], in_=src)
+                    nc.vector.tensor_copy(out=dst, in_=src)
                 else:
-                    nc.scalar.copy(out=half[:, i, :, :, :], in_=src)
+                    nc.scalar.copy(out=dst, in_=src)
             flat = half[:].rearrange("p i a n j -> p (i a n j)")
             codes = w_codes[:].rearrange("p i a n -> p (i a n)")
             scales = w_scales[:].rearrange("p i a n -> p (i a n)")
@@ -100,8 +113,11 @@ def tile_routed_moe_kernel(tc, xT, w, b, gate, offs, out):
                     scales=scales[:, c0:c1],
                     in_=flat[:, PACK * c0 : PACK * c1],
                 )
-            acc = sums.tile([P, 2, C], F32)
-            y = ys.tile([P, 2 * C], F32)
+            return w_codes, w_scales
+
+        def finish(e0, w_codes, w_scales):
+            acc = sums.tile([P, 2, C], F32, name="acc")
+            y = ys.tile([P, 2 * C], F32, name="y")
             for i in range(2):
                 cols = slice((e0 + i) * C, (e0 + i + 1) * C)
                 for a in range(PASSES):
@@ -114,16 +130,30 @@ def tile_routed_moe_kernel(tc, xT, w, b, gate, offs, out):
                         start=(a == 0),
                         stop=(a == PASSES - 1),
                     )
-                nc.vector.scalar_tensor_tensor(
+                nc.scalar.activation(
                     out=y[:, i * C : (i + 1) * C],
-                    in0=acc[:, i, :],
-                    scalar=bias[:, e0 + i : e0 + i + 1],
-                    in1=gates[:, cols],
-                    op0=ADD,
-                    op1=MULT,
+                    in_=acc[:, i, :],
+                    func=mybir.ActivationFunctionType.Identity,
+                    bias=bias_of(e0 + i),
                 )
-            nc.vector.tensor_copy(
+            nc.vector.tensor_tensor(
                 out=result[:].indirect(slots[:, e0 * C // 16 : (e0 + 2) * C // 16]),
-                in_=y[:],
+                in0=y[:],
+                in1=gates[:, e0 * C : (e0 + 2) * C],
+                op=MULT,
             )
+
+        ready = []
+        for e0 in range(0, E, 2):
+            ready.append((e0, *prepare(e0)))
+            for g in GATES_AFTER.get(e0, ()):
+                cols = slice(g * GATE_COLS, (g + 1) * GATE_COLS)
+                nc.sync.dma_start(gates[:, cols], gate[:, cols])
+            if e0 in BIAS_AFTER:
+                i0, i1 = BIAS_AFTER[e0]
+                nc.sync.dma_start(biases[e0][:], b[:, i0:i1])
+            while len(ready) > LAG.get(e0, E):
+                finish(*ready.pop(0))
+        for one in ready:
+            finish(*one)
         nc.sync.dma_start(out, result[:])

@@ -19,14 +19,14 @@ LINE = 4
 K_PASS = P * PACK
 PASSES = K // K_PASS
 UNIT = 512
-CHUNKS = ((512, 512, 512, 512), (1024, 1024), (1024, 512, 512))
-X_VECTOR = {(0, 1), (0, 3), (1, 3), (2, 3)}
-W_VECTOR = set()
+CHUNKS = ((1024, 1024), (1024, 1024), (1024, 512, 512))
+X_VECTOR = {(0, 1): 512, (0, 3): 512, (1, 3): 512, (2, 3): 512}
+W_GPSIMD = {1, 3, 5, 7}
 GATHER = 1024
 GATE_COLS = 1024
-GATES_AFTER = {6: (0,), 10: (1,)}
-BIAS_AFTER = {10: (0, 12), 14: (12, 16)}
-LAG = {10: 0, 14: 0}
+GATES_AFTER = {8: (0, 1)}
+BIAS_AFTER = {8: (0, 10), 14: (10, 16)}
+LAG = {8: 0, 14: 0}
 
 
 def tile_routed_moe_kernel(tc, xT, w, b, gate, offs, out):
@@ -65,10 +65,11 @@ def tile_routed_moe_kernel(tc, xT, w, b, gate, offs, out):
                     half = halves.tile([P, UNIT, PACK], BF16, name="half", align_bytes=64)
                     src = raw[:, :, o : o + UNIT].rearrange("p j (c i) -> p c j i", i=LINE)
                     dst = half[:].rearrange("p (c i) j -> p c j i", i=LINE)
-                    if (a, (t0 + o) // UNIT) in X_VECTOR:
-                        nc.vector.tensor_copy(out=dst, in_=src)
-                    else:
-                        nc.scalar.copy(out=dst, in_=src)
+                    v = X_VECTOR.get((a, (t0 + o) // UNIT), 0) // LINE
+                    if v > 0:
+                        nc.vector.tensor_copy(out=dst[:, :v], in_=src[:, :v])
+                    if v < UNIT // LINE:
+                        nc.scalar.copy(out=dst[:, v:], in_=src[:, v:])
                     cols = slice(t0 + o, t0 + o + UNIT)
                     nc.vector.quantize_mx(
                         out=x_codes[a][:, cols].bitcast(FP8X4),
@@ -100,8 +101,15 @@ def tile_routed_moe_kernel(tc, xT, w, b, gate, offs, out):
                 )
                 src = raw[:, i, :, :, :].rearrange("p a j (c i) -> p a c j i", i=LINE)
                 dst = half[:, i, :, :, :].rearrange("p a (c i) j -> p a c j i", i=LINE)
-                if e0 + i in W_VECTOR:
-                    nc.vector.tensor_copy(out=dst, in_=src)
+                if e0 + i in W_GPSIMD:
+                    nc.gpsimd.tensor_scalar(
+                        out=half[:, i, :, :, :],
+                        in0=raw[:, i, :, :, :].rearrange("p a j n -> p a n j"),
+                        scalar1=1.0,
+                        scalar2=0.0,
+                        op0=MULT,
+                        op1=mybir.AluOpType.add,
+                    )
                 else:
                     nc.scalar.copy(out=dst, in_=src)
             flat = half[:].rearrange("p i a n j -> p (i a n j)")

from contextlib import ExitStack

import concourse.mybir as mybir

K, T, E, C, N = 1536, 2048, 16, 128, 128
FLOPS = 2 * K * T * N

F32 = mybir.dt.float32
BF16 = mybir.dt.bfloat16
U32 = mybir.dt.uint32
U16 = mybir.dt.uint16
U8 = mybir.dt.uint8
FP8X4 = mybir.dt.float8_e4m3fn_x4
MULT = mybir.AluOpType.mult

P = 128
PACK = 4
LINE = 4
K_PASS = P * PACK
PASSES = K // K_PASS
UNIT = 512
CHUNKS = ((1024, 1024), (1024, 1024), (1024, 512, 512))
X_VECTOR = {(0, 1): 512, (0, 3): 512, (1, 3): 512, (2, 3): 512}
W_GPSIMD = {1, 3, 5, 7}
GATHER = 1024
GATE_COLS = 1024
GATES_AFTER = {8: (0, 1)}
BIAS_AFTER = {8: (0, 10), 14: (10, 16)}
LAG = {8: 0, 14: 0}


def tile_routed_moe_kernel(tc, xT, w, b, gate, offs, out):
    nc = tc.nc
    with ExitStack() as ctx:
        keep = ctx.enter_context(tc.tile_pool(name="keep", bufs=1))
        raws = ctx.enter_context(tc.tile_pool(name="raws", bufs=5))
        halves = ctx.enter_context(tc.tile_pool(name="halves", bufs=6))
        sums = ctx.enter_context(tc.psum_pool(name="sums", bufs=8))
        ys = ctx.enter_context(tc.tile_pool(name="ys", bufs=8))

        slots = keep.tile([P, T // 16], U16)
        nc.sync.dma_start(slots[:], offs)
        x_codes = [keep.tile([P, T], U32, name=f"x_codes{a}", align_bytes=64) for a in range(PASSES)]
        x_scales = keep.tile([P, T], U8, align_bytes=64)
        g_codes = [keep.tile([P, T], U32, name=f"g_codes{a}", align_bytes=64) for a in range(PASSES)]
        g_scales = keep.tile([P, T], U8, align_bytes=64)
        nc.gpsimd.memset(x_scales[:], 0)
        biases = {e0: keep.tile([P, i1 - i0], F32, name=f"bias{e0}") for e0, (i0, i1) in BIAS_AFTER.items()}
        gates = keep.tile([P, E * C], F32)
        result = keep.tile([P, T], F32)

        def gather(out_tile, window, s):
            nc.vector.tensor_copy(
                out=out_tile[:, s : s + GATHER],
                in_=window[:].indirect(slots[:, s // 16 : (s + GATHER) // 16]),
            )

        for a in range(PASSES):
            rows = xT[a * K_PASS : (a + 1) * K_PASS, :].rearrange("(p j) n -> p j n", j=PACK)
            t0 = 0
            for width in CHUNKS[a]:
                raw = raws.tile([P, PACK, width], F32, name="raw")
                nc.sync.dma_start(raw[:], rows[:, :, t0 : t0 + width])
                for o in range(0, width, UNIT):
                    half = halves.tile([P, UNIT, PACK], BF16, name="half", align_bytes=64)
                    src = raw[:, :, o : o + UNIT].rearrange("p j (c i) -> p c j i", i=LINE)
                    dst = half[:].rearrange("p (c i) j -> p c j i", i=LINE)
                    v = X_VECTOR.get((a, (t0 + o) // UNIT), 0) // LINE
                    if v > 0:
                        nc.vector.tensor_copy(out=dst[:, :v], in_=src[:, :v])
                    if v < UNIT // LINE:
                        nc.scalar.copy(out=dst[:, v:], in_=src[:, v:])
                    cols = slice(t0 + o, t0 + o + UNIT)
                    nc.vector.quantize_mx(
                        out=x_codes[a][:, cols].bitcast(FP8X4),
                        scales=x_scales[4 * a :, cols],
                        in_=half[:].rearrange("p n j -> p (n j)"),
                    )
                t0 += width
            if a < PASSES - 1:
                for s in range(0, T, GATHER):
                    gather(g_codes[a], x_codes[a], s)
        for s in range(0, T, GATHER):
            gather(g_codes[PASSES - 1], x_codes[PASSES - 1], s)
            gather(g_scales, x_scales, s)

        def bias_of(e):
            for key, (i0, i1) in BIAS_AFTER.items():
                if i0 <= e < i1:
                    return biases[key][:, e - i0 : e - i0 + 1]

        def prepare(e0):
            raw = raws.tile([P, 2, PASSES, PACK, N], F32, name="raw")
            half = halves.tile([P, 2, PASSES, N, PACK], BF16, name="half", align_bytes=64)
            w_codes = keep.tile([P, 2, PASSES, N], U32, name=f"w_codes{e0}", align_bytes=64)
            w_scales = keep.tile([P, 2, PASSES, N], U8, name=f"w_scales{e0}", align_bytes=64)
            for i in range(2):
                nc.sync.dma_start(
                    raw[:, i, :, :, :].rearrange("p a j n -> p a (j n)"),
                    w[e0 + i, :, :].rearrange("(a p j) n -> p a (j n)", p=P, j=PACK),
                )
                src = raw[:, i, :, :, :].rearrange("p a j (c i) -> p a c j i", i=LINE)
                dst = half[:, i, :, :, :].rearrange("p a (c i) j -> p a c j i", i=LINE)
                if e0 + i in W_GPSIMD:
                    nc.gpsimd.tensor_scalar(
                        out=half[:, i, :, :, :],
                        in0=raw[:, i, :, :, :].rearrange("p a j n -> p a n j"),
                        scalar1=1.0,
                        scalar2=0.0,
                        op0=MULT,
                        op1=mybir.AluOpType.add,
                    )
                else:
                    nc.scalar.copy(out=dst, in_=src)
            flat = half[:].rearrange("p i a n j -> p (i a n j)")
            codes = w_codes[:].rearrange("p i a n -> p (i a n)")
            scales = w_scales[:].rearrange("p i a n -> p (i a n)")
            for c0, c1 in ((0, 512), (512, 768)):
                nc.vector.quantize_mx(
                    out=codes[:, c0:c1].bitcast(FP8X4),
                    scales=scales[:, c0:c1],
                    in_=flat[:, PACK * c0 : PACK * c1],
                )
            return w_codes, w_scales

        def finish(e0, w_codes, w_scales):
            acc = sums.tile([P, 2, C], F32, name="acc")
            y = ys.tile([P, 2 * C], F32, name="y")
            for i in range(2):
                cols = slice((e0 + i) * C, (e0 + i + 1) * C)
                for a in range(PASSES):
                    nc.tensor.matmul_mx(
                        out=acc[:, i, :],
                        lhsT=w_codes[:, i, a, :].bitcast(FP8X4),
                        lhsT_scale=w_scales[:, i, a, :],
                        rhs=g_codes[a][:, cols].bitcast(FP8X4),
                        rhs_scale=g_scales[4 * a :, cols],
                        start=(a == 0),
                        stop=(a == PASSES - 1),
                    )
                nc.scalar.activation(
                    out=y[:, i * C : (i + 1) * C],
                    in_=acc[:, i, :],
                    func=mybir.ActivationFunctionType.Identity,
                    bias=bias_of(e0 + i),
                )
            nc.vector.tensor_tensor(
                out=result[:].indirect(slots[:, e0 * C // 16 : (e0 + 2) * C // 16]),
                in0=y[:],
                in1=gates[:, e0 * C : (e0 + 2) * C],
                op=MULT,
            )

        ready = []
        for e0 in range(0, E, 2):
            ready.append((e0, *prepare(e0)))
            for g in GATES_AFTER.get(e0, ()):
                cols = slice(g * GATE_COLS, (g + 1) * GATE_COLS)
                nc.sync.dma_start(gates[:, cols], gate[:, cols])
            if e0 in BIAS_AFTER:
                i0, i1 = BIAS_AFTER[e0]
                nc.sync.dma_start(biases[e0][:], b[:, i0:i1])
            while len(ready) > LAG.get(e0, E):
                finish(*ready.pop(0))
        for one in ready:
            finish(*one)
        nc.sync.dma_start(out, result[:])
